import numpy as np
import ml_dtypes


def mxq(x, axis, fmt="e4m3"):
    dtype, down = {"e4m3": (ml_dtypes.float8_e4m3fn, 7), "e5m2": (ml_dtypes.float8_e5m2, 14)}[fmt]
    v = np.moveaxis(np.asarray(x, np.float32).astype(ml_dtypes.bfloat16).astype(np.float64), axis, -1)
    blocks = v.reshape(v.shape[:-1] + (-1, 32))
    amax = np.abs(blocks).max(-1, keepdims=True)
    byte = np.maximum(np.where(amax > 0, np.frexp(amax)[1] - 1 + 127, 0) - down, 1)
    scale = np.exp2(byte - 127.0)
    codes = (blocks / scale).astype(np.float32).astype(dtype).astype(np.float64)
    return np.moveaxis((codes * scale).reshape(v.shape), -1, axis)


WIDE = False


def mx_kscale(k, group=512):
    if not WIDE:
        return np.ones(k)
    levels = np.array([10, -10, 5, -5, 0])
    if group != 512:
        return np.exp2(np.random.permutation(np.resize(levels, k // group))).repeat(group)
    if k % 512:
        return np.exp2(np.random.permutation(np.resize(levels, k // 32))).repeat(32)
    a = np.empty((k // 512, 16))
    for p in range(k // 512):
        a[p, :8] = np.random.permutation(np.resize(levels, 8))
        for g in range(8):
            far = levels[np.abs(levels - a[p, g]) >= 10]
            a[p, g + 8] = far[np.random.randint(len(far))]
    return np.exp2(a.ravel()).repeat(32)


def f64(x):
    return np.asarray(x).astype(np.float64)


def gelu(v):
    return 0.5 * v * (1.0 + np.tanh(0.7978845608028654 * (v + 0.044715 * v ** 3)))


G, D, M, N = 4, 256, 128, 1024


def setup_inputs():
    n = np.random.standard_normal
    s = mx_kscale(D, 0)[:, None]
    return {
        "x": (n((G, D, N)) * s).astype(np.float32),
        "w": (n((G, D, M)) / np.sqrt(D) / s).astype(np.float32),
        "u": (n((G, D, M)) / np.sqrt(D) / s).astype(np.float32),
        "r": n((G, M, N)).astype(np.float32),
    }


def reference(x, w, u, r):
    xq = mxq(f64(x), 1, "e4m3")
    h = mxq(f64(w), 1, "e4m3").transpose(0, 2, 1) @ xq
    g = mxq(f64(u), 1, "e4m3").transpose(0, 2, 1) @ xq
    y = gelu(h) * g
    y = y + f64(r)
    return y

@@ -1,0 +1,124 @@
+from contextlib import ExitStack
+
+import concourse.mybir as mybir
+
+G, D, M, N = 4, 256, 128, 1024
+FLOPS = 2 * 2 * G * D * M * N
+
+F32 = mybir.dt.float32
+BF16 = mybir.dt.bfloat16
+U32 = mybir.dt.uint32
+U8 = mybir.dt.uint8
+FP8X4 = mybir.dt.float8_e4m3fn_x4
+GELU = mybir.ActivationFunctionType.Gelu_apprx_tanh
+ALU = mybir.AluOpType
+
+P = 128
+PACK = 4
+ROWS = 64
+COLS = 512
+RUN = 4
+SHARE = [320,288,352,224]
+LOADS = "X0 w0 u0 X1 X2 w1 u1 R0 X3 R1 R2 R3".split()
+ORDER = "cV0 cS0 wS0 uS0 qx0 qw0 mm0 cV1 cS1 qx1 mm1 ge00 ge01 cV2 cS2 wS1 uS1 mu00 mu01 qx2 qw1 mm2 ge10 ge11 ad00 ad01 mu10 mu11 cV3 cS3 ad10 qx3 mm3 ad11 ge20 ge21 mu20 mu21 ad20 ad21 ge30 ge31 mu30 mu31 ad30 ad31".split()
+
+
+def tile_rows_gglu_gelu_res_kernel(tc, x, w, u, r, out):
+    nc = tc.nc
+    x_rows = x.rearrange("g d n -> (g d) n")
+    weights = {"w": w.rearrange("g d m -> (g d) m"), "u": u.rearrange("g d m -> (g d) m")}
+
+    with ExitStack() as ctx:
+        sb = ctx.enter_context(tc.tile_pool(name="sb", bufs=1))
+        ps = ctx.enter_context(tc.psum_pool(name="ps", bufs=1))
+        ctx.enter_context(tc.manual_schedule())
+
+        x_raw = [sb.tile([P, PACK, COLS], F32, name="x_raw%d" % t, align_bytes=64) for t in range(4)]
+        x_bf = [sb.tile([P, COLS * PACK], BF16, name="x_bf%d" % t, align_bytes=64) for t in range(4)]
+        x_codes = [sb.tile([P, COLS], U32, name="x_codes%d" % t, align_bytes=64) for t in range(4)]
+        x_scales = [sb.tile([P, COLS], U8, name="x_scales%d" % t, align_bytes=64) for t in range(4)]
+        w_raw = {(k, p): sb.tile([P, PACK, M], F32, name="raw_%s%d" % (k, p), align_bytes=64) for k in "wu" for p in range(2)}
+        w_bf = [sb.tile([P, 2 * M * PACK], BF16, name="w_bf%d" % p, align_bytes=64) for p in range(2)]
+        w_codes = [sb.tile([P, 2 * M], U32, name="w_codes%d" % p, align_bytes=64) for p in range(2)]
+        w_scales = [sb.tile([P, 2 * M], U8, name="w_scales%d" % p, align_bytes=64) for p in range(2)]
+        res = [sb.tile([P, 2, COLS], F32, name="res%d" % t, align_bytes=64) for t in range(4)]
+        act = {(t, c): sb.tile([P, COLS], F32, name="act%d%d" % (t, c), align_bytes=64) for t in range(4) for c in range(2)}
+        prod = {(t, c): sb.tile([P, COLS], F32, name="prod%d%d" % (t, c), align_bytes=64) for t in range(4) for c in range(2)}
+        y = {(t, c): sb.tile([P, COLS], F32, name="y%d%d" % (t, c), align_bytes=64) for t in range(4) for c in range(2)}
+        banks = {(k, c, h): ps.tile([P, COLS], F32, name="bank_%s%d%d" % (k, c, h)) for k in "wu" for c in range(2) for h in range(2)}
+
+        def cols_of(t):
+            return slice((t % 2) * COLS, (t % 2 + 1) * COLS)
+
+        def load(name):
+            kind, t = name[0], int(name[1])
+            if kind == "X":
+                rows = x_rows[(t // 2) * P * PACK : (t // 2 + 1) * P * PACK, cols_of(t)]
+                nc.sync.dma_start(out=x_raw[t][:], in_=rows.rearrange("(p j) n -> p j n", j=PACK))
+            elif kind == "R":
+                rows = r[2 * (t // 2) : 2 * (t // 2) + 2, :, cols_of(t)]
+                nc.sync.dma_start(out=res[t][:], in_=rows.rearrange("c m n -> m c n"))
+            else:
+                rows = weights[kind][t * P * PACK : (t + 1) * P * PACK, :]
+                nc.sync.dma_start(out=w_raw[kind, t][:], in_=rows.rearrange("(p j) m -> p j m", j=PACK))
+
+        def interleave(on_vector, dst, src):
+            dst = dst.rearrange("p (c i t) -> p c t i", i=RUN, t=PACK)
+            src = src.rearrange("p t (c i) -> p c t i", i=RUN)
+            if on_vector:
+                nc.vector.tensor_copy(out=dst, in_=src)
+            else:
+                nc.scalar.copy(out=dst, in_=src)
+
+        def quantize(codes, scales, values):
+            nc.vector.quantize_mx(out=codes[:].bitcast(FP8X4), scales=scales[:], in_=values[:])
+
+        def products(t):
+            pair = t // 2
+            for i, k in enumerate("wu"):
+                for c in range(2):
+                    rows = slice(c * ROWS, (c + 1) * ROWS)
+                    m_cols = slice(i * M, (i + 1) * M)
+                    nc.tensor.matmul_mx(
+                        out=banks[k, c, t % 2][:],
+                        lhsT=w_codes[pair][rows, m_cols].bitcast(FP8X4),
+                        lhsT_scale=w_scales[pair][rows, m_cols],
+                        rhs=x_codes[t][rows, :].bitcast(FP8X4),
+                        rhs_scale=x_scales[t][rows, :],
+                        start=True,
+                        stop=True,
+                    )
+
+        def step(name):
+            kind = name[:2]
+            if kind in ("wV", "wS", "uV", "uS"):
+                p = int(name[2])
+                i = 0 if name[0] == "w" else 1
+                interleave(name[1] == "V", w_bf[p][:, i * M * PACK : (i + 1) * M * PACK], w_raw[name[0], p][:])
+                return
+            t = int(name[2])
+            if kind == "cV":
+                interleave(True, x_bf[t][:, : SHARE[t] * PACK], x_raw[t][:, :, : SHARE[t]])
+            elif kind == "cS":
+                interleave(False, x_bf[t][:, SHARE[t] * PACK :], x_raw[t][:, :, SHARE[t] :])
+            elif kind == "qx":
+                quantize(x_codes[t], x_scales[t], x_bf[t])
+            elif kind == "qw":
+                quantize(w_codes[t], w_scales[t], w_bf[t])
+            elif kind == "mm":
+                products(t)
+            else:
+                c = int(name[3])
+                if kind == "ge":
+                    nc.scalar.activation(out=act[t, c][:], in_=banks["w", c, t % 2][:], func=GELU)
+                elif kind == "mu":
+                    nc.vector.tensor_tensor(out=prod[t, c][:], in0=banks["u", c, t % 2][:], in1=act[t, c][:], op=ALU.mult)
+                else:
+                    eng = nc.vector if kind == "ad" else nc.gpsimd
+                    eng.tensor_tensor(out=y[t, c][:], in0=prod[t, c][:], in1=res[t][:, c, :], op=ALU.add)
+                    nc.sync.dma_start(out=out[2 * (t // 2) + c, :, cols_of(t)], in_=y[t, c][:])
+
+        for name in LOADS:
+            load(name)
+        for name in ORDER:
+            step(name)

@@ -18,9 +18,8 @@ PACK = 4
 ROWS = 64
 COLS = 512
 RUN = 4
-SHARE = [320,288,352,224]
-LOADS = "X0 w0 u0 X1 X2 w1 u1 R0 X3 R1 R2 R3".split()
-ORDER = "cV0 cS0 wS0 uS0 qx0 qw0 mm0 cV1 cS1 qx1 mm1 ge00 ge01 cV2 cS2 wS1 uS1 mu00 mu01 qx2 qw1 mm2 ge10 ge11 ad00 ad01 mu10 mu11 cV3 cS3 ad10 qx3 mm3 ad11 ge20 ge21 mu20 mu21 ad20 ad21 ge30 ge31 mu30 mu31 ad30 ad31".split()
+SHARE = [512,416,352,320]
+ORDER = "X0 w0 u0 X1 w1 u1 X2 G0 X3 G1 G2 G3 cV0 qx0 wS0 uS0 qw0 cV1 mh00 mh01 mg00 mg01 ge00 cS1 ge01 wS1 uS1 mu00 qx1 mu01 qw1 cV2 mh10 mh11 mg10 mg11 ge10 cS2 ge11 mu10 qx2 mu11 ad00 ad10 cV3 mh20 mh21 mg20 mg21 S0 ge20 cS3 ge21 mu20 qx3 mu21 ad01 ad11 ad20 ad21 mh30 mh31 mg30 mg31 S1 s20 s21 ge30 ge31 mu30 mu31 ad30 ad31 s30 s31".split()
 
 
 def tile_rows_gglu_gelu_res_kernel(tc, x, w, u, r, out):
@@ -41,10 +40,10 @@ def tile_rows_gglu_gelu_res_kernel(tc, x, w, u, r, out):
         w_bf = [sb.tile([P, 2 * M * PACK], BF16, name="w_bf%d" % p, align_bytes=64) for p in range(2)]
         w_codes = [sb.tile([P, 2 * M], U32, name="w_codes%d" % p, align_bytes=64) for p in range(2)]
         w_scales = [sb.tile([P, 2 * M], U8, name="w_scales%d" % p, align_bytes=64) for p in range(2)]
-        res = [sb.tile([P, 2, COLS], F32, name="res%d" % t, align_bytes=64) for t in range(4)]
+        res = [sb.tile([P, N], F32, name="res%d" % g, align_bytes=64) for g in range(G)]
         act = {(t, c): sb.tile([P, COLS], F32, name="act%d%d" % (t, c), align_bytes=64) for t in range(4) for c in range(2)}
         prod = {(t, c): sb.tile([P, COLS], F32, name="prod%d%d" % (t, c), align_bytes=64) for t in range(4) for c in range(2)}
-        y = {(t, c): sb.tile([P, COLS], F32, name="y%d%d" % (t, c), align_bytes=64) for t in range(4) for c in range(2)}
+        y = [sb.tile([P, N], F32, name="y%d" % g, align_bytes=64) for g in range(G)]
         banks = {(k, c, h): ps.tile([P, COLS], F32, name="bank_%s%d%d" % (k, c, h)) for k in "wu" for c in range(2) for h in range(2)}
 
         def cols_of(t):
@@ -55,9 +54,8 @@ def tile_rows_gglu_gelu_res_kernel(tc, x, w, u, r, out):
             if kind == "X":
                 rows = x_rows[(t // 2) * P * PACK : (t // 2 + 1) * P * PACK, cols_of(t)]
                 nc.sync.dma_start(out=x_raw[t][:], in_=rows.rearrange("(p j) n -> p j n", j=PACK))
-            elif kind == "R":
-                rows = r[2 * (t // 2) : 2 * (t // 2) + 2, :, cols_of(t)]
-                nc.sync.dma_start(out=res[t][:], in_=rows.rearrange("c m n -> m c n"))
+            elif kind == "G":
+                nc.sync.dma_start(out=res[t][:], in_=r[t])
             else:
                 rows = weights[kind][t * P * PACK : (t + 1) * P * PACK, :]
                 nc.sync.dma_start(out=w_raw[kind, t][:], in_=rows.rearrange("(p j) m -> p j m", j=PACK))
@@ -73,24 +71,32 @@ def tile_rows_gglu_gelu_res_kernel(tc, x, w, u, r, out):
         def quantize(codes, scales, values):
             nc.vector.quantize_mx(out=codes[:].bitcast(FP8X4), scales=scales[:], in_=values[:])
 
-        def products(t):
-            pair = t // 2
-            for i, k in enumerate("wu"):
-                for c in range(2):
-                    rows = slice(c * ROWS, (c + 1) * ROWS)
-                    m_cols = slice(i * M, (i + 1) * M)
-                    nc.tensor.matmul_mx(
-                        out=banks[k, c, t % 2][:],
-                        lhsT=w_codes[pair][rows, m_cols].bitcast(FP8X4),
-                        lhsT_scale=w_scales[pair][rows, m_cols],
-                        rhs=x_codes[t][rows, :].bitcast(FP8X4),
-                        rhs_scale=x_scales[t][rows, :],
-                        start=True,
-                        stop=True,
-                    )
+        def product(k, t, c):
+            pair, i = t // 2, (1 if k == "u" else 0)
+            rows = slice(c * ROWS, (c + 1) * ROWS)
+            m_cols = slice(i * M, (i + 1) * M)
+            nc.tensor.matmul_mx(
+                out=banks[k, c, t % 2][:],
+                lhsT=w_codes[pair][rows, m_cols].bitcast(FP8X4),
+                lhsT_scale=w_scales[pair][rows, m_cols],
+                rhs=x_codes[t][rows, :].bitcast(FP8X4),
+                rhs_scale=x_scales[t][rows, :],
+                start=True,
+                stop=True,
+            )
 
         def step(name):
             kind = name[:2]
+            if len(name) == 2 and name[0] != "S":
+                load(name)
+                return
+            if name[0] == "S":
+                nc.sync.dma_start(out=out[int(name[1])], in_=y[int(name[1])][:])
+                return
+            if name[0] == "s":
+                t, c = int(name[1]), int(name[2])
+                nc.sync.dma_start(out=out[2 * (t // 2) + c, :, cols_of(t)], in_=y[2 * (t // 2) + c][:, cols_of(t)])
+                return
             if kind in ("wV", "wS", "uV", "uS"):
                 p = int(name[2])
                 i = 0 if name[0] == "w" else 1
@@ -105,20 +111,17 @@ def tile_rows_gglu_gelu_res_kernel(tc, x, w, u, r, out):
                 quantize(x_codes[t], x_scales[t], x_bf[t])
             elif kind == "qw":
                 quantize(w_codes[t], w_scales[t], w_bf[t])
-            elif kind == "mm":
-                products(t)
             else:
                 c = int(name[3])
-                if kind == "ge":
+                if kind in ("mh", "mg"):
+                    product("w" if kind == "mh" else "u", t, c)
+                elif kind == "ge":
                     nc.scalar.activation(out=act[t, c][:], in_=banks["w", c, t % 2][:], func=GELU)
                 elif kind == "mu":
                     nc.vector.tensor_tensor(out=prod[t, c][:], in0=banks["u", c, t % 2][:], in1=act[t, c][:], op=ALU.mult)
                 else:
-                    eng = nc.vector if kind == "ad" else nc.gpsimd
-                    eng.tensor_tensor(out=y[t, c][:], in0=prod[t, c][:], in1=res[t][:, c, :], op=ALU.add)
-                    nc.sync.dma_start(out=out[2 * (t // 2) + c, :, cols_of(t)], in_=y[t, c][:])
+                    g = 2 * (t // 2) + c
+                    nc.vector.tensor_tensor(out=y[g][:, cols_of(t)], in0=prod[t, c][:], in1=res[g][:, cols_of(t)], op=ALU.add)
 
-        for name in LOADS:
-            load(name)
         for name in ORDER:
             step(name)

@@ -17,9 +17,9 @@ P = 128
 PACK = 4
 ROWS = 64
 COLS = 512
-RUN = 4
-SHARE = [512,416,352,320]
-ORDER = "X0 w0 u0 X1 w1 u1 X2 G0 X3 G1 G2 G3 cV0 qx0 wS0 uS0 qw0 cV1 mh00 mh01 mg00 mg01 ge00 cS1 ge01 wS1 uS1 mu00 qx1 mu01 qw1 cV2 mh10 mh11 mg10 mg11 ge10 cS2 ge11 mu10 qx2 mu11 ad00 ad10 cV3 mh20 mh21 mg20 mg21 S0 ge20 cS3 ge21 mu20 qx3 mu21 ad01 ad11 ad20 ad21 mh30 mh31 mg30 mg31 S1 s20 s21 ge30 ge31 mu30 mu31 ad30 ad31 s30 s31".split()
+RUN = 2
+SHARE = [512,384,352,256]
+ORDER = "X0 w0 u0 X1 X2 w1 u1 G0 X3 G1 G2 G3 cV0 qx0 wS0 uS0 qw0 cV1 mh00 mh01 mg00 mg01 ge00 cS1 ge01 cS2 wS1 mu00 qx1 mu01 cV2 uV1 qx2 qw1 mh10 mh11 mg10 mg11 mh20 mh21 mg20 mg21 ge10 ge11 ge20 ge21 cS3 mu10 mu11 ad00 ad10 mu20 cV3 mu21 qx3 ad01 ad11 ad20 ad21 mh30 mh31 mg30 mg31 S0 S1 s20 s21 ge30 ge31 mu30 mu31 ad30 ad31 s30 s31".split()
 
 
 def tile_rows_gglu_gelu_res_kernel(tc, x, w, u, r, out):

@@ -18,8 +18,9 @@ PACK = 4
 ROWS = 64
 COLS = 512
 RUN = 2
-SHARE = [512,384,352,256]
-ORDER = "X0 w0 u0 X1 X2 w1 u1 G0 X3 G1 G2 G3 cV0 qx0 wS0 uS0 qw0 cV1 mh00 mh01 mg00 mg01 ge00 cS1 ge01 cS2 wS1 mu00 qx1 mu01 cV2 uV1 qx2 qw1 mh10 mh11 mg10 mg11 mh20 mh21 mg20 mg21 ge10 ge11 ge20 ge21 cS3 mu10 mu11 ad00 ad10 mu20 cV3 mu21 qx3 ad01 ad11 ad20 ad21 mh30 mh31 mg30 mg31 S0 S1 s20 s21 ge30 ge31 mu30 mu31 ad30 ad31 s30 s31".split()
+SHARE = [512,384,352,224]
+ON_GPSIMD = ["ad01","ad21"]
+ORDER = "X0 w0 u0 X1 X2 w1 u1 X3 G0 G1 G2 G3 cV0 qx0 wS0 uS0 qw0 cV1 mh00 mh01 mg00 mg01 ge00 cS1 ge01 cS2 wS1 mu00 qx1 mu01 cV2 uV1 qx2 qw1 mh10 mh11 mg10 mg11 mh20 mh21 mg20 mg21 ge10 ge11 cS3 ge20 ge21 mu10 mu11 cV3 ad00 ad10 ad01 qx3 mu20 mu21 ad11 ad21 ad20 mh30 mh31 mg30 mg31 S0 S1 s20 s21 ge30 ge31 mu30 mu31 ad30 ad31 s30 s31".split()
 
 
 def tile_rows_gglu_gelu_res_kernel(tc, x, w, u, r, out):
@@ -42,8 +43,11 @@ def tile_rows_gglu_gelu_res_kernel(tc, x, w, u, r, out):
         w_scales = [sb.tile([P, 2 * M], U8, name="w_scales%d" % p, align_bytes=64) for p in range(2)]
         res = [sb.tile([P, N], F32, name="res%d" % g, align_bytes=64) for g in range(G)]
         act = {(t, c): sb.tile([P, COLS], F32, name="act%d%d" % (t, c), align_bytes=64) for t in range(4) for c in range(2)}
-        prod = {(t, c): sb.tile([P, COLS], F32, name="prod%d%d" % (t, c), align_bytes=64) for t in range(4) for c in range(2)}
         y = [sb.tile([P, N], F32, name="y%d" % g, align_bytes=64) for g in range(G)]
+        prod = {(t, c): sb.tile([P, COLS], F32, name="prod%d%d" % (t, c), align_bytes=64) for t in (0, 2, 3) for c in range(2)}
+        prod = {key: prod[key][:] for key in prod}
+        for c in range(2):
+            prod[1, c] = y[2 * c + 1][:, :COLS]
         banks = {(k, c, h): ps.tile([P, COLS], F32, name="bank_%s%d%d" % (k, c, h)) for k in "wu" for c in range(2) for h in range(2)}
 
         def cols_of(t):
@@ -118,10 +122,10 @@ def tile_rows_gglu_gelu_res_kernel(tc, x, w, u, r, out):
                 elif kind == "ge":
                     nc.scalar.activation(out=act[t, c][:], in_=banks["w", c, t % 2][:], func=GELU)
                 elif kind == "mu":
-                    nc.vector.tensor_tensor(out=prod[t, c][:], in0=banks["u", c, t % 2][:], in1=act[t, c][:], op=ALU.mult)
+                    nc.vector.tensor_tensor(out=prod[t, c], in0=banks["u", c, t % 2][:], in1=act[t, c][:], op=ALU.mult)
                 else:
                     g = 2 * (t // 2) + c
-                    nc.vector.tensor_tensor(out=y[g][:, cols_of(t)], in0=prod[t, c][:], in1=res[g][:, cols_of(t)], op=ALU.add)
+                    (nc.gpsimd if name in ON_GPSIMD else nc.vector).tensor_tensor(out=y[g][:, cols_of(t)], in0=prod[t, c], in1=res[g][:, cols_of(t)], op=ALU.add)
 
         for name in ORDER:
             step(name)

from contextlib import ExitStack

import concourse.mybir as mybir

G, D, M, N = 4, 256, 128, 1024
FLOPS = 2 * 2 * G * D * M * N

F32 = mybir.dt.float32
BF16 = mybir.dt.bfloat16
U32 = mybir.dt.uint32
U8 = mybir.dt.uint8
FP8X4 = mybir.dt.float8_e4m3fn_x4
GELU = mybir.ActivationFunctionType.Gelu_apprx_tanh
ALU = mybir.AluOpType

P = 128
PACK = 4
ROWS = 64
COLS = 512
RUN = 2
SHARE = [512,384,352,224]
ON_GPSIMD = ["ad01","ad21"]
ORDER = "X0 w0 u0 X1 X2 w1 u1 X3 G0 G1 G2 G3 cV0 qx0 wS0 uS0 qw0 cV1 mh00 mh01 mg00 mg01 ge00 cS1 ge01 cS2 wS1 mu00 qx1 mu01 cV2 uV1 qx2 qw1 mh10 mh11 mg10 mg11 mh20 mh21 mg20 mg21 ge10 ge11 cS3 ge20 ge21 mu10 mu11 cV3 ad00 ad10 ad01 qx3 mu20 mu21 ad11 ad21 ad20 mh30 mh31 mg30 mg31 S0 S1 s20 s21 ge30 ge31 mu30 mu31 ad30 ad31 s30 s31".split()


def tile_rows_gglu_gelu_res_kernel(tc, x, w, u, r, out):
    nc = tc.nc
    x_rows = x.rearrange("g d n -> (g d) n")
    weights = {"w": w.rearrange("g d m -> (g d) m"), "u": u.rearrange("g d m -> (g d) m")}

    with ExitStack() as ctx:
        sb = ctx.enter_context(tc.tile_pool(name="sb", bufs=1))
        ps = ctx.enter_context(tc.psum_pool(name="ps", bufs=1))
        ctx.enter_context(tc.manual_schedule())

        x_raw = [sb.tile([P, PACK, COLS], F32, name="x_raw%d" % t, align_bytes=64) for t in range(4)]
        x_bf = [sb.tile([P, COLS * PACK], BF16, name="x_bf%d" % t, align_bytes=64) for t in range(4)]
        x_codes = [sb.tile([P, COLS], U32, name="x_codes%d" % t, align_bytes=64) for t in range(4)]
        x_scales = [sb.tile([P, COLS], U8, name="x_scales%d" % t, align_bytes=64) for t in range(4)]
        w_raw = {(k, p): sb.tile([P, PACK, M], F32, name="raw_%s%d" % (k, p), align_bytes=64) for k in "wu" for p in range(2)}
        w_bf = [sb.tile([P, 2 * M * PACK], BF16, name="w_bf%d" % p, align_bytes=64) for p in range(2)]
        w_codes = [sb.tile([P, 2 * M], U32, name="w_codes%d" % p, align_bytes=64) for p in range(2)]
        w_scales = [sb.tile([P, 2 * M], U8, name="w_scales%d" % p, align_bytes=64) for p in range(2)]
        res = [sb.tile([P, N], F32, name="res%d" % g, align_bytes=64) for g in range(G)]
        act = {(t, c): sb.tile([P, COLS], F32, name="act%d%d" % (t, c), align_bytes=64) for t in range(4) for c in range(2)}
        y = [sb.tile([P, N], F32, name="y%d" % g, align_bytes=64) for g in range(G)]
        prod = {(t, c): sb.tile([P, COLS], F32, name="prod%d%d" % (t, c), align_bytes=64) for t in (0, 2, 3) for c in range(2)}
        prod = {key: prod[key][:] for key in prod}
        for c in range(2):
            prod[1, c] = y[2 * c + 1][:, :COLS]
        banks = {(k, c, h): ps.tile([P, COLS], F32, name="bank_%s%d%d" % (k, c, h)) for k in "wu" for c in range(2) for h in range(2)}

        def cols_of(t):
            return slice((t % 2) * COLS, (t % 2 + 1) * COLS)

        def load(name):
            kind, t = name[0], int(name[1])
            if kind == "X":
                rows = x_rows[(t // 2) * P * PACK : (t // 2 + 1) * P * PACK, cols_of(t)]
                nc.sync.dma_start(out=x_raw[t][:], in_=rows.rearrange("(p j) n -> p j n", j=PACK))
            elif kind == "G":
                nc.sync.dma_start(out=res[t][:], in_=r[t])
            else:
                rows = weights[kind][t * P * PACK : (t + 1) * P * PACK, :]
                nc.sync.dma_start(out=w_raw[kind, t][:], in_=rows.rearrange("(p j) m -> p j m", j=PACK))

        def interleave(on_vector, dst, src):
            dst = dst.rearrange("p (c i t) -> p c t i", i=RUN, t=PACK)
            src = src.rearrange("p t (c i) -> p c t i", i=RUN)
            if on_vector:
                nc.vector.tensor_copy(out=dst, in_=src)
            else:
                nc.scalar.copy(out=dst, in_=src)

        def quantize(codes, scales, values):
            nc.vector.quantize_mx(out=codes[:].bitcast(FP8X4), scales=scales[:], in_=values[:])

        def product(k, t, c):
            pair, i = t // 2, (1 if k == "u" else 0)
            rows = slice(c * ROWS, (c + 1) * ROWS)
            m_cols = slice(i * M, (i + 1) * M)
            nc.tensor.matmul_mx(
                out=banks[k, c, t % 2][:],
                lhsT=w_codes[pair][rows, m_cols].bitcast(FP8X4),
                lhsT_scale=w_scales[pair][rows, m_cols],
                rhs=x_codes[t][rows, :].bitcast(FP8X4),
                rhs_scale=x_scales[t][rows, :],
                start=True,
                stop=True,
            )

        def step(name):
            kind = name[:2]
            if len(name) == 2 and name[0] != "S":
                load(name)
                return
            if name[0] == "S":
                nc.sync.dma_start(out=out[int(name[1])], in_=y[int(name[1])][:])
                return
            if name[0] == "s":
                t, c = int(name[1]), int(name[2])
                nc.sync.dma_start(out=out[2 * (t // 2) + c, :, cols_of(t)], in_=y[2 * (t // 2) + c][:, cols_of(t)])
                return
            if kind in ("wV", "wS", "uV", "uS"):
                p = int(name[2])
                i = 0 if name[0] == "w" else 1
                interleave(name[1] == "V", w_bf[p][:, i * M * PACK : (i + 1) * M * PACK], w_raw[name[0], p][:])
                return
            t = int(name[2])
            if kind == "cV":
                interleave(True, x_bf[t][:, : SHARE[t] * PACK], x_raw[t][:, :, : SHARE[t]])
            elif kind == "cS":
                interleave(False, x_bf[t][:, SHARE[t] * PACK :], x_raw[t][:, :, SHARE[t] :])
            elif kind == "qx":
                quantize(x_codes[t], x_scales[t], x_bf[t])
            elif kind == "qw":
                quantize(w_codes[t], w_scales[t], w_bf[t])
            else:
                c = int(name[3])
                if kind in ("mh", "mg"):
                    product("w" if kind == "mh" else "u", t, c)
                elif kind == "ge":
                    nc.scalar.activation(out=act[t, c][:], in_=banks["w", c, t % 2][:], func=GELU)
                elif kind == "mu":
                    nc.vector.tensor_tensor(out=prod[t, c], in0=banks["u", c, t % 2][:], in1=act[t, c][:], op=ALU.mult)
                else:
                    g = 2 * (t // 2) + c
                    (nc.gpsimd if name in ON_GPSIMD else nc.vector).tensor_tensor(out=y[g][:, cols_of(t)], in0=prod[t, c], in1=res[g][:, cols_of(t)], op=ALU.add)

        for name in ORDER:
            step(name)
